import numpy as np
import ml_dtypes


def mxq(x, axis, fmt="e4m3"):
    dtype, down = {"e4m3": (ml_dtypes.float8_e4m3fn, 7), "e5m2": (ml_dtypes.float8_e5m2, 14)}[fmt]
    v = np.moveaxis(np.asarray(x, np.float32).astype(ml_dtypes.bfloat16).astype(np.float64), axis, -1)
    blocks = v.reshape(v.shape[:-1] + (-1, 32))
    amax = np.abs(blocks).max(-1, keepdims=True)
    byte = np.maximum(np.where(amax > 0, np.frexp(amax)[1] - 1 + 127, 0) - down, 1)
    scale = np.exp2(byte - 127.0)
    codes = (blocks / scale).astype(np.float32).astype(dtype).astype(np.float64)
    return np.moveaxis((codes * scale).reshape(v.shape), -1, axis)


WIDE = False


def mx_kscale(k):
    if not WIDE:
        return np.ones(k)
    levels = np.array([10, -10, 5, -5, 0])
    if k % 512:
        return np.exp2(np.random.permutation(np.resize(levels, k // 32))).repeat(32)
    a = np.empty((k // 512, 16))
    for p in range(k // 512):
        a[p, :8] = np.random.permutation(np.resize(levels, 8))
        for g in range(8):
            far = levels[np.abs(levels - a[p, g]) >= 10]
            a[p, g + 8] = far[np.random.randint(len(far))]
    return np.exp2(a.ravel()).repeat(32)


def f64(x):
    return np.asarray(x).astype(np.float64)


def striped(idx):
    return np.tile(np.asarray(idx).reshape(-1, 16).T, (8, 1)).astype(np.uint16)


def unstriped(offs):
    return offs[:16].T.reshape(-1).astype(np.int64)


E2M1 = np.array([0.0, 0.5, 1.0, 1.5, 2.0, 3.0, 4.0, 6.0, -0.0, -0.5, -1.0, -1.5, -2.0, -3.0, -4.0, -6.0])


def pack_weight(w, fmt):
    k, n = w.shape
    w = f64(np.asarray(w, np.float32).astype(ml_dtypes.bfloat16)).reshape(k // 32, 32, n)
    amax = np.abs(w).max(1)
    if fmt == "e4m3":
        byte = np.frexp(amax)[1] - 1 + 127 - 7
    else:
        mant, ex = np.frexp(amax / 6.0)
        byte = np.where(mant > 0.5, ex, ex - 1) + 127
    byte = np.clip(np.where(amax > 0, byte, 1), 1, 254)
    scaled = (w * np.exp2(127.0 - byte)[:, None, :]).reshape(k, n).astype(np.float32)
    by_word = np.ascontiguousarray(scaled.reshape(k // 512, 128, 4, n).transpose(0, 1, 3, 2))
    if fmt == "e4m3":
        words = by_word.astype(ml_dtypes.float8_e4m3fn).view(np.uint8)
    else:
        c = by_word.astype(ml_dtypes.float4_e2m1fn).view(np.uint8) & 0xF
        words = (c[..., 0::2] | (c[..., 1::2] << 4)).reshape(k // 512, 128, 2 * n)
    return np.ascontiguousarray(words), np.ascontiguousarray(byte.astype(np.uint8).reshape(k // 512, 16, n))


def unpack_weight(words, scales, fmt):
    g, _, n = scales.shape
    words = np.ascontiguousarray(words).reshape(g, 128, n, -1)
    if fmt == "e4m3":
        vals = words.view(ml_dtypes.float8_e4m3fn).astype(np.float64)
    else:
        nib = np.empty((g, 128, n, 4), np.uint8)
        nib[..., 0::2] = words & 0xF
        nib[..., 1::2] = words >> 4
        vals = E2M1[nib]
    vals = vals * np.repeat(np.exp2(scales.astype(np.float64) - 127.0), 8, axis=1)[..., None]
    return vals.transpose(0, 1, 3, 2).reshape(g * 512, n)


K, T, J, B, N = 512, 2048, 2048, 512, 512


def setup_inputs():
    n = np.random.standard_normal
    idx = np.random.randint(0, T, J)
    fk = mx_kscale(K)
    wap = pack_weight(n((K, N)) * 1 / np.sqrt(K) / fk[:, None], "e2m1")
    wbp = pack_weight(n((K, N)) * 1 / np.sqrt(K) / fk[:, None], "e4m3")
    return {
        "xt": (n((K, T))).astype(np.float32),
        "fa": (np.random.uniform(0.5, 2.0, (K, 1)) * fk[:, None]).astype(np.float32),
        "fb": (np.random.uniform(0.5, 2.0, (K, 1)) * fk[:, None]).astype(np.float32),
        "wa_words": wap[0],
        "wa_scales": wap[1],
        "wb_words": wbp[0],
        "wb_scales": wbp[1],
        "offs": striped(idx),
    }


def reference(xt, fa, fb, wa_words, wa_scales, wb_words, wb_scales, offs):
    idx = unstriped(offs)
    wau = unpack_weight(wa_words, wa_scales, "e2m1")
    wbu = unpack_weight(wb_words, wb_scales, "e4m3")
    m = f64(xt)[:, idx].reshape(K, B, J // B).mean(axis=2)
    mr = np.repeat(m, J // B, axis=1)
    d = np.square(f64(xt)[:, idx] - mr)
    u = d.reshape(K, B, J // B).mean(axis=2) * f64(fa)
    v = m * f64(fb)
    uq = mxq(u, 0, "e4m3")
    vq = mxq(v, 0, "e4m3")
    y = wau.T @ uq + wbu.T @ vq
    return y

@@ -1,0 +1,230 @@
+import math
+from contextlib import ExitStack
+
+import concourse.mybir as mybir
+from concourse.masks import make_identity
+
+K, T, J, B, N = 512, 2048, 2048, 512, 512
+FLOPS = 2 * 2 * K * N * B
+
+F32 = mybir.dt.float32
+BF16 = mybir.dt.bfloat16
+I32 = mybir.dt.int32
+U32 = mybir.dt.uint32
+U16 = mybir.dt.uint16
+U8 = mybir.dt.uint8
+FP8X4 = mybir.dt.float8_e4m3fn_x4
+FP4X4 = mybir.dt.float4_e2m1fn_x4
+ACT = mybir.ActivationFunctionType
+ALU = mybir.AluOpType
+
+P = 128
+PACK = 4
+GROUP = J // B
+CHUNK = 128
+HALF = 256
+
+
+G_BUFS = 3
+M_BUFS = 3
+LEAD = 2
+ON_VECTOR = (1, 5)
+LAG_U = 1
+LAG_W = 2
+LAG_S = 3
+ORDER = 0
+
+
+def tile_list_group_spread_kernel(tc, xt, fa, fb, wa_words, wa_scales, wb_words, wb_scales, offs, out):
+    nc = tc.nc
+    with ExitStack() as ctx:
+        held = ctx.enter_context(tc.tile_pool(name="held", bufs=1))
+        gathered = ctx.enter_context(tc.tile_pool(name="gathered", bufs=G_BUFS))
+        ring = ctx.enter_context(tc.tile_pool(name="ring", bufs=M_BUFS))
+        late = ctx.enter_context(tc.tile_pool(name="late", bufs=2))
+        sums = ctx.enter_context(tc.psum_pool(name="sums", bufs=1))
+        psum = ctx.enter_context(tc.psum_pool(name="psum", bufs=2))
+
+        offsets = held.tile([P, J // 16], U16, name="offsets")
+        planes = [held.tile([P, T], F32, name="plane%d" % t) for t in range(PACK)]
+        ident = held.tile([P, P], F32, name="ident")
+        fa_t = held.tile([P, PACK], F32, name="fa_t")
+        fb_t = held.tile([P, PACK], F32, name="fb_t")
+        fa_row = held.tile([P, 2, P, 2], F32, name="fa_row")
+        fb_quarter = held.tile([P, PACK], F32, name="fb_quarter")
+        wa = held.tile([P, 2 * N], U8, name="wa", align_bytes=64)
+        wb = held.tile([P, 4 * N], U8, name="wb", align_bytes=64)
+        wa_s = held.tile([P, N], U8, name="wa_s", align_bytes=64)
+        wb_s = held.tile([P, N], U8, name="wb_s", align_bytes=64)
+        total = [held.tile([P, PACK, HALF], F32, name="total%d" % h) for h in range(2)]
+        spread = [sums.tile([P, PACK, P], F32, name="spread%d" % c) for c in range(B // CHUNK)]
+
+        xt_planes = xt.rearrange("(p t) n -> t p n", t=PACK)
+        nc.scalar.dma_start(out=fa_t[:], in_=fa.rearrange("(p t) o -> p (t o)", t=PACK))
+        nc.scalar.dma_start(out=fb_t[:], in_=fb.rearrange("(p t) o -> p (t o)", t=PACK))
+        nc.sync.dma_start(offsets[:], offs)
+        for t in range(PACK):
+            nc.sync.dma_start(out=planes[t][:], in_=xt_planes[t])
+        nc.sync.dma_start(out=wa[:].bitcast(I32), in_=wa_words[0].bitcast(I32))
+        nc.sync.dma_start(out=wb[:].bitcast(I32), in_=wb_words[0].rearrange("p n t -> p (n t)").bitcast(I32))
+        make_identity(nc, ident[:])
+        for plane, scales in ((wa_s, wa_scales), (wb_s, wb_scales)):
+            nc.gpsimd.memset(plane[:].bitcast(I32), 0)
+            for q in range(4):
+                nc.sync.dma_start(
+                    out=plane[32 * q : 32 * q + 4, :].bitcast(I32),
+                    in_=scales[0, 4 * q : 4 * q + 4, :].bitcast(I32),
+                )
+        nc.scalar.activation(out=fb_quarter[:], in_=fb_t[:], func=ACT.Copy, scale=0.25)
+        fa_turned = psum.tile([P, PACK, P], F32, name="turned")
+        for t in range(PACK):
+            nc.tensor.transpose(fa_turned[:, t, :], fa_t[:, t : t + 1].to_broadcast([P, P]), ident[:])
+        nc.vector.tensor_copy(out=fa_row[:], in_=fa_turned[:].rearrange("b (u e) p -> b u p e", e=2))
+
+        halves = [((t,), h * HALF, HALF) for t in range(2) for h in range(2)]
+        quarters = [((2, 3), c * CHUNK, CHUNK) for c in range(4)]
+        items = [
+            halves[:3] + quarters[:2] + halves[3:] + quarters[2:],
+            halves + quarters,
+            halves[:3] + quarters[:1] + halves[3:] + quarters[1:],
+        ][ORDER]
+        n_items = len(items)
+        closes = {i: items[i][1] // CHUNK for i in range(n_items) if len(items[i][0]) == 2}
+        made = {}
+
+        def gather(i):
+            ts, b0, nb = items[i]
+            g = gathered.tile([P, GROUP * HALF], F32, name="g%d" % i, tag="g")
+            cols = offsets[:, b0 * GROUP // 16 : (b0 + nb) * GROUP // 16]
+            for s, t in enumerate(ts):
+                dst = g[:, s * nb * GROUP : (s + 1) * nb * GROUP]
+                if i in ON_VECTOR:
+                    nc.vector.tensor_copy(out=dst, in_=planes[t][:].indirect(cols))
+                else:
+                    nc.scalar.activation(out=dst, in_=planes[t][:].indirect(cols), func=ACT.Copy)
+            made["g", i] = g
+
+        def linear(i):
+            ts, b0, nb = items[i]
+            g = made["g", i][:].rearrange("p (b j) -> p b j", j=GROUP)
+            both = ring.tile([P, HALF, 2], F32, name="both%d" % i, tag="both")
+            diff = ring.tile([P, HALF, 2], F32, name="diff%d" % i, tag="diff")
+            odd = ring.tile([P, HALF], F32, name="odd%d" % i, tag="odd")
+            nc.vector.tensor_tensor(out=both[:], in0=g[:, :, 0:2], in1=g[:, :, 2:4], op=ALU.add)
+            nc.vector.tensor_tensor(out=diff[:], in0=g[:, :, 0:2], in1=g[:, :, 2:4], op=ALU.subtract)
+            nc.vector.tensor_tensor(out=odd[:], in0=both[:, :, 0], in1=both[:, :, 1], op=ALU.subtract)
+            nc.vector.tensor_tensor(
+                out=total[b0 // HALF][:, ts[0] : ts[-1] + 1, b0 % HALF : b0 % HALF + nb],
+                in0=both[:, :, 0].rearrange("p (t b) -> p t b", t=len(ts)),
+                in1=both[:, :, 1].rearrange("p (t b) -> p t b", t=len(ts)),
+                op=ALU.add,
+            )
+            made["diff", i] = diff
+            made["odd", i] = odd
+
+        def squares(i):
+            ts, b0, nb = items[i]
+            diff_sq = ring.tile([P, HALF, 2], F32, name="diff_sq%d" % i, tag="diff_sq")
+            odd_sq = ring.tile([P, HALF], F32, name="odd_sq%d" % i, tag="odd_sq")
+            nc.scalar.activation(out=diff_sq[:], in_=made["diff", i][:], func=ACT.Square, scale=math.sqrt(0.125))
+            nc.scalar.activation(out=odd_sq[:], in_=made["odd", i][:], func=ACT.Square, scale=0.25)
+            for s in range(HALF // CHUNK):
+                t = ts[s * CHUNK // nb]
+                c = (b0 + s * CHUNK % nb) // CHUNK
+                cols = slice(s * CHUNK, (s + 1) * CHUNK)
+                terms = (diff_sq[:, cols, 0], diff_sq[:, cols, 1], odd_sq[:, cols])
+                for n, term in enumerate(terms):
+                    nc.tensor.matmul(
+                        out=spread[c][:, t, :],
+                        lhsT=term,
+                        rhs=ident[:],
+                        start=(n == 0),
+                        stop=(n == len(terms) - 1),
+                        is_transpose=True,
+                    )
+
+        def round_mean(c):
+            b0 = c * CHUNK
+            rounded = late.tile([P, 2, CHUNK * PACK], BF16, name="rounded%d" % c, tag="rounded", align_bytes=64)
+            src = total[b0 // HALF][:, :, b0 % HALF : b0 % HALF + CHUNK]
+            nc.vector.tensor_tensor(
+                out=rounded[:, 1, :].rearrange("p (c i t) -> p c t i", i=2, t=PACK),
+                in0=src.rearrange("p t (c i) -> p c t i", i=2),
+                in1=fb_quarter[:].unsqueeze(1).unsqueeze(3).to_broadcast([P, CHUNK // 2, PACK, 2]),
+                op=ALU.mult,
+            )
+            made["rounded", c] = rounded
+
+        def round_spread(c):
+            pairs = late.tile([P, 2, P, 2], BF16, name="pairs%d" % c, tag="pairs")
+            nc.vector.tensor_tensor(
+                out=pairs[:],
+                in0=spread[c][:].rearrange("b (u e) p -> b u p e", e=2),
+                in1=fa_row[:],
+                op=ALU.mult,
+            )
+            words = pairs[:].rearrange("b u p e -> b u (p e)").bitcast(F32)
+            turned = psum.tile([P, PACK, P], F32, name="turned%d" % c, tag="turned")
+            for u in range(2):
+                nc.tensor.transpose(turned[:, u, :], words[:, u, :], ident[:])
+            made["turned", c] = turned
+
+        def product(c):
+            rounded = made["rounded", c]
+            nc.scalar.copy(
+                out=rounded[:, 0, :].bitcast(F32).rearrange("p (b u) -> p b u", u=2),
+                in_=made["turned", c][:, 0:2, :].rearrange("p u b -> p b u"),
+            )
+            codes = late.tile([P, 2, CHUNK], U32, name="codes%d" % c, tag="codes", align_bytes=64)
+            scales = late.tile([P, 2, CHUNK], U8, name="scales%d" % c, tag="scales", align_bytes=64)
+            nc.vector.quantize_mx(
+                out=codes[:].rearrange("p s b -> p (s b)").bitcast(FP8X4),
+                scales=scales[:].rearrange("p s b -> p (s b)"),
+                in_=rounded[:].rearrange("p s b -> p (s b)"),
+            )
+            acc = psum.tile([P, N // P, CHUNK], F32, name="acc%d" % c, tag="acc")
+            for a in range(N // P):
+                nc.tensor.matmul_mx(
+                    out=acc[:, a, :],
+                    lhsT=wa[:, 2 * P * a : 2 * P * (a + 1)].bitcast(FP4X4),
+                    lhsT_scale=wa_s[:, P * a : P * (a + 1)],
+                    rhs=codes[:, 0, :].bitcast(FP8X4),
+                    rhs_scale=scales[:, 0, :],
+                    start=True,
+                    stop=False,
+                )
+                nc.tensor.matmul_mx(
+                    out=acc[:, a, :],
+                    lhsT=wb[:, 4 * P * a : 4 * P * (a + 1)].bitcast(FP8X4),
+                    lhsT_scale=wb_s[:, P * a : P * (a + 1)],
+                    rhs=codes[:, 1, :].bitcast(FP8X4),
+                    rhs_scale=scales[:, 1, :],
+                    start=False,
+                    stop=True,
+                )
+            made["acc", c] = acc
+
+        def store(c):
+            result = late.tile([P, N // P, CHUNK], F32, name="result%d" % c, tag="result")
+            nc.scalar.copy(out=result[:], in_=made["acc", c][:])
+            nc.sync.dma_start(
+                out=out.rearrange("(a p) b -> p a b", p=P)[:, :, c * CHUNK : (c + 1) * CHUNK], in_=result[:]
+            )
+
+        for i in range(LEAD):
+            gather(i)
+        for i in range(n_items + LAG_S):
+            if i + LEAD < n_items:
+                gather(i + LEAD)
+            if i < n_items:
+                linear(i)
+            if i in closes:
+                round_mean(closes[i])
+            if i - LAG_U in closes:
+                round_spread(closes[i - LAG_U])
+            if i < n_items:
+                squares(i)
+            if i - LAG_W in closes:
+                product(closes[i - LAG_W])
+            if i - LAG_S in closes:
+                store(closes[i - LAG_S])

@@ -26,13 +26,19 @@ HALF = 256
 
 
 G_BUFS = 3
-M_BUFS = 3
+M_BUFS = 5
 LEAD = 2
-ON_VECTOR = (1, 5)
+ON_VECTOR = {1: 2, 4: 2}
+SPLIT_LAST = 1
+SPLIT_OUT = (3,)
 LAG_U = 1
 LAG_W = 2
 LAG_S = 3
-ORDER = 0
+ORDER = 1
+WORDS_ON_VECTOR = ()
+OUT_ON_VECTOR = ()
+LAG_M = 1
+T_BUFS = 1
 
 
 def tile_list_group_spread_kernel(tc, xt, fa, fb, wa_words, wa_scales, wb_words, wb_scales, offs, out):
@@ -41,16 +47,16 @@ def tile_list_group_spread_kernel(tc, xt, fa, fb, wa_words, wa_scales, wb_words,
         held = ctx.enter_context(tc.tile_pool(name="held", bufs=1))
         gathered = ctx.enter_context(tc.tile_pool(name="gathered", bufs=G_BUFS))
         ring = ctx.enter_context(tc.tile_pool(name="ring", bufs=M_BUFS))
-        late = ctx.enter_context(tc.tile_pool(name="late", bufs=2))
+        late = ctx.enter_context(tc.tile_pool(name="late", bufs=4))
         sums = ctx.enter_context(tc.psum_pool(name="sums", bufs=1))
-        psum = ctx.enter_context(tc.psum_pool(name="psum", bufs=2))
+        turn = ctx.enter_context(tc.psum_pool(name="turn", bufs=T_BUFS))
+        psum = ctx.enter_context(tc.psum_pool(name="psum", bufs=4 - T_BUFS))
 
         offsets = held.tile([P, J // 16], U16, name="offsets")
         planes = [held.tile([P, T], F32, name="plane%d" % t) for t in range(PACK)]
         ident = held.tile([P, P], F32, name="ident")
-        fa_t = held.tile([P, PACK], F32, name="fa_t")
         fb_t = held.tile([P, PACK], F32, name="fb_t")
-        fa_row = held.tile([P, 2, P, 2], F32, name="fa_row")
+        fa_row = held.tile([P, K], F32, name="fa_row")
         fb_quarter = held.tile([P, PACK], F32, name="fb_quarter")
         wa = held.tile([P, 2 * N], U8, name="wa", align_bytes=64)
         wb = held.tile([P, 4 * N], U8, name="wb", align_bytes=64)
@@ -60,13 +66,13 @@ def tile_list_group_spread_kernel(tc, xt, fa, fb, wa_words, wa_scales, wb_words,
         spread = [sums.tile([P, PACK, P], F32, name="spread%d" % c) for c in range(B // CHUNK)]
 
         xt_planes = xt.rearrange("(p t) n -> t p n", t=PACK)
-        nc.scalar.dma_start(out=fa_t[:], in_=fa.rearrange("(p t) o -> p (t o)", t=PACK))
         nc.scalar.dma_start(out=fb_t[:], in_=fb.rearrange("(p t) o -> p (t o)", t=PACK))
         nc.sync.dma_start(offsets[:], offs)
         for t in range(PACK):
             nc.sync.dma_start(out=planes[t][:], in_=xt_planes[t])
         nc.sync.dma_start(out=wa[:].bitcast(I32), in_=wa_words[0].bitcast(I32))
         nc.sync.dma_start(out=wb[:].bitcast(I32), in_=wb_words[0].rearrange("p n t -> p (n t)").bitcast(I32))
+        nc.sync.dma_start(out=fa_row[:], in_=fa.rearrange("k o -> (k o)").partition_broadcast(P))
         make_identity(nc, ident[:])
         for plane, scales in ((wa_s, wa_scales), (wb_s, wb_scales)):
             nc.gpsimd.memset(plane[:].bitcast(I32), 0)
@@ -76,40 +82,47 @@ def tile_list_group_spread_kernel(tc, xt, fa, fb, wa_words, wa_scales, wb_words,
                     in_=scales[0, 4 * q : 4 * q + 4, :].bitcast(I32),
                 )
         nc.scalar.activation(out=fb_quarter[:], in_=fb_t[:], func=ACT.Copy, scale=0.25)
-        fa_turned = psum.tile([P, PACK, P], F32, name="turned")
-        for t in range(PACK):
-            nc.tensor.transpose(fa_turned[:, t, :], fa_t[:, t : t + 1].to_broadcast([P, P]), ident[:])
-        nc.vector.tensor_copy(out=fa_row[:], in_=fa_turned[:].rearrange("b (u e) p -> b u p e", e=2))
 
         halves = [((t,), h * HALF, HALF) for t in range(2) for h in range(2)]
         quarters = [((2, 3), c * CHUNK, CHUNK) for c in range(4)]
+        if SPLIT_LAST:
+            quarters = quarters[:3] + [((2,), 3 * CHUNK, CHUNK), ((3,), 3 * CHUNK, CHUNK)]
         items = [
             halves[:3] + quarters[:2] + halves[3:] + quarters[2:],
             halves + quarters,
             halves[:3] + quarters[:1] + halves[3:] + quarters[1:],
         ][ORDER]
         n_items = len(items)
-        closes = {i: items[i][1] // CHUNK for i in range(n_items) if len(items[i][0]) == 2}
+        closes = {i: items[i][1] // CHUNK for i in range(n_items) if 3 in items[i][0]}
         made = {}
 
         def gather(i):
             ts, b0, nb = items[i]
-            g = gathered.tile([P, GROUP * HALF], F32, name="g%d" % i, tag="g")
-            cols = offsets[:, b0 * GROUP // 16 : (b0 + nb) * GROUP // 16]
-            for s, t in enumerate(ts):
-                dst = g[:, s * nb * GROUP : (s + 1) * nb * GROUP]
-                if i in ON_VECTOR:
-                    nc.vector.tensor_copy(out=dst, in_=planes[t][:].indirect(cols))
+            g = gathered.tile([P, GROUP * nb * len(ts)], F32, name="g%d" % i, tag="g")
+            share = ON_VECTOR.get(i, 0)
+            if len(ts) == 1:
+                cut = nb - share * CHUNK
+                parts = [(ts[0], 0, cut, False), (ts[0], cut, nb, True)]
+            else:
+                parts = [(t, 0, nb, s >= len(ts) - share) for s, t in enumerate(ts)]
+            for t, lo, hi, on_vector in parts:
+                if lo == hi:
+                    continue
+                at = (t - ts[0]) * nb
+                dst = g[:, (at + lo) * GROUP : (at + hi) * GROUP]
+                window = planes[t][:].indirect(offsets[:, (b0 + lo) * GROUP // 16 : (b0 + hi) * GROUP // 16])
+                if on_vector:
+                    nc.vector.tensor_copy(out=dst, in_=window)
                 else:
-                    nc.scalar.activation(out=dst, in_=planes[t][:].indirect(cols), func=ACT.Copy)
+                    nc.scalar.activation(out=dst, in_=window, func=ACT.Copy)
             made["g", i] = g
 
         def linear(i):
             ts, b0, nb = items[i]
             g = made["g", i][:].rearrange("p (b j) -> p b j", j=GROUP)
-            both = ring.tile([P, HALF, 2], F32, name="both%d" % i, tag="both")
-            diff = ring.tile([P, HALF, 2], F32, name="diff%d" % i, tag="diff")
-            odd = ring.tile([P, HALF], F32, name="odd%d" % i, tag="odd")
+            both = ring.tile([P, nb * len(ts), 2], F32, name="both%d" % i, tag="both")
+            diff = ring.tile([P, nb * len(ts), 2], F32, name="diff%d" % i, tag="diff")
+            odd = ring.tile([P, nb * len(ts)], F32, name="odd%d" % i, tag="odd")
             nc.vector.tensor_tensor(out=both[:], in0=g[:, :, 0:2], in1=g[:, :, 2:4], op=ALU.add)
             nc.vector.tensor_tensor(out=diff[:], in0=g[:, :, 0:2], in1=g[:, :, 2:4], op=ALU.subtract)
             nc.vector.tensor_tensor(out=odd[:], in0=both[:, :, 0], in1=both[:, :, 1], op=ALU.subtract)
@@ -124,11 +137,11 @@ def tile_list_group_spread_kernel(tc, xt, fa, fb, wa_words, wa_scales, wb_words,
 
         def squares(i):
             ts, b0, nb = items[i]
-            diff_sq = ring.tile([P, HALF, 2], F32, name="diff_sq%d" % i, tag="diff_sq")
-            odd_sq = ring.tile([P, HALF], F32, name="odd_sq%d" % i, tag="odd_sq")
+            diff_sq = ring.tile([P, nb * len(ts), 2], F32, name="diff_sq%d" % i, tag="diff_sq")
+            odd_sq = ring.tile([P, nb * len(ts)], F32, name="odd_sq%d" % i, tag="odd_sq")
             nc.scalar.activation(out=diff_sq[:], in_=made["diff", i][:], func=ACT.Square, scale=math.sqrt(0.125))
             nc.scalar.activation(out=odd_sq[:], in_=made["odd", i][:], func=ACT.Square, scale=0.25)
-            for s in range(HALF // CHUNK):
+            for s in range(nb * len(ts) // CHUNK):
                 t = ts[s * CHUNK // nb]
                 c = (b0 + s * CHUNK % nb) // CHUNK
                 cols = slice(s * CHUNK, (s + 1) * CHUNK)
@@ -143,73 +156,86 @@ def tile_list_group_spread_kernel(tc, xt, fa, fb, wa_words, wa_scales, wb_words,
                         is_transpose=True,
                     )
 
+        def quantize(rounded, key, c):
+            codes = late.tile([P, CHUNK], U32, name="codes_%s%d" % (key, c), tag="codes_" + key, align_bytes=64)
+            scales = late.tile([P, CHUNK], U8, name="scales_%s%d" % (key, c), tag="scales_" + key, align_bytes=64)
+            nc.vector.quantize_mx(out=codes[:].bitcast(FP8X4), scales=scales[:], in_=rounded[:])
+            return codes, scales
+
         def round_mean(c):
             b0 = c * CHUNK
-            rounded = late.tile([P, 2, CHUNK * PACK], BF16, name="rounded%d" % c, tag="rounded", align_bytes=64)
+            rounded = late.tile([P, CHUNK * PACK], BF16, name="v%d" % c, tag="v", align_bytes=64)
             src = total[b0 // HALF][:, :, b0 % HALF : b0 % HALF + CHUNK]
             nc.vector.tensor_tensor(
-                out=rounded[:, 1, :].rearrange("p (c i t) -> p c t i", i=2, t=PACK),
+                out=rounded[:].rearrange("p (c i t) -> p c t i", i=2, t=PACK),
                 in0=src.rearrange("p t (c i) -> p c t i", i=2),
                 in1=fb_quarter[:].unsqueeze(1).unsqueeze(3).to_broadcast([P, CHUNK // 2, PACK, 2]),
                 op=ALU.mult,
             )
-            made["rounded", c] = rounded
+            made["v", c] = rounded
 
         def round_spread(c):
             pairs = late.tile([P, 2, P, 2], BF16, name="pairs%d" % c, tag="pairs")
             nc.vector.tensor_tensor(
                 out=pairs[:],
                 in0=spread[c][:].rearrange("b (u e) p -> b u p e", e=2),
-                in1=fa_row[:],
+                in1=fa_row[:].rearrange("b (p u e) -> b u p e", u=2, e=2),
                 op=ALU.mult,
             )
             words = pairs[:].rearrange("b u p e -> b u (p e)").bitcast(F32)
-            turned = psum.tile([P, PACK, P], F32, name="turned%d" % c, tag="turned")
+            turned = turn.tile([P, PACK, P], F32, name="turned%d" % c, tag="turned")
             for u in range(2):
                 nc.tensor.transpose(turned[:, u, :], words[:, u, :], ident[:])
             made["turned", c] = turned
 
-        def product(c):
-            rounded = made["rounded", c]
-            nc.scalar.copy(
-                out=rounded[:, 0, :].bitcast(F32).rearrange("p (b u) -> p b u", u=2),
-                in_=made["turned", c][:, 0:2, :].rearrange("p u b -> p b u"),
-            )
-            codes = late.tile([P, 2, CHUNK], U32, name="codes%d" % c, tag="codes", align_bytes=64)
-            scales = late.tile([P, 2, CHUNK], U8, name="scales%d" % c, tag="scales", align_bytes=64)
-            nc.vector.quantize_mx(
-                out=codes[:].rearrange("p s b -> p (s b)").bitcast(FP8X4),
-                scales=scales[:].rearrange("p s b -> p (s b)"),
-                in_=rounded[:].rearrange("p s b -> p (s b)"),
-            )
-            acc = psum.tile([P, N // P, CHUNK], F32, name="acc%d" % c, tag="acc")
+        def product_mean(c):
+            codes, scales = quantize(made["v", c], "v", c)
+            n_parts = 2 if c in SPLIT_OUT else 1
+            per = N // P // n_parts
+            acc = [psum.tile([P, per, CHUNK], F32, name="acc%d_%d" % (c, s), tag="acc") for s in range(n_parts)]
             for a in range(N // P):
                 nc.tensor.matmul_mx(
-                    out=acc[:, a, :],
-                    lhsT=wa[:, 2 * P * a : 2 * P * (a + 1)].bitcast(FP4X4),
-                    lhsT_scale=wa_s[:, P * a : P * (a + 1)],
-                    rhs=codes[:, 0, :].bitcast(FP8X4),
-                    rhs_scale=scales[:, 0, :],
-                    start=True,
-                    stop=False,
-                )
-                nc.tensor.matmul_mx(
-                    out=acc[:, a, :],
+                    out=acc[a // per][:, a % per, :],
                     lhsT=wb[:, 4 * P * a : 4 * P * (a + 1)].bitcast(FP8X4),
                     lhsT_scale=wb_s[:, P * a : P * (a + 1)],
-                    rhs=codes[:, 1, :].bitcast(FP8X4),
-                    rhs_scale=scales[:, 1, :],
-                    start=False,
-                    stop=True,
+                    rhs=codes[:].bitcast(FP8X4),
+                    rhs_scale=scales[:],
+                    start=(a % per == 0),
+                    stop=False,
                 )
             made["acc", c] = acc
 
-        def store(c):
-            result = late.tile([P, N // P, CHUNK], F32, name="result%d" % c, tag="result")
-            nc.scalar.copy(out=result[:], in_=made["acc", c][:])
-            nc.sync.dma_start(
-                out=out.rearrange("(a p) b -> p a b", p=P)[:, :, c * CHUNK : (c + 1) * CHUNK], in_=result[:]
+        def product_spread(c):
+            rounded = late.tile([P, CHUNK * PACK], BF16, name="u%d" % c, tag="u", align_bytes=64)
+            copy = nc.vector.tensor_copy if c in WORDS_ON_VECTOR else nc.scalar.copy
+            copy(
+                out=rounded[:].bitcast(F32).rearrange("p (b u) -> p b u", u=2),
+                in_=made["turned", c][:, 0:2, :].rearrange("p u b -> p b u"),
             )
+            codes, scales = quantize(rounded, "u", c)
+            acc = made["acc", c]
+            per = N // P // len(acc)
+            for a in range(N // P):
+                nc.tensor.matmul_mx(
+                    out=acc[a // per][:, a % per, :],
+                    lhsT=wa[:, 2 * P * a : 2 * P * (a + 1)].bitcast(FP4X4),
+                    lhsT_scale=wa_s[:, P * a : P * (a + 1)],
+                    rhs=codes[:].bitcast(FP8X4),
+                    rhs_scale=scales[:],
+                    start=False,
+                    stop=(a % per == per - 1),
+                )
+
+        def store(c):
+            acc = made["acc", c]
+            per = N // P // len(acc)
+            for s, part in enumerate(acc):
+                result = late.tile([P, per, CHUNK], F32, name="result%d_%d" % (c, s), tag="result")
+                on_vector = (c in OUT_ON_VECTOR) != (s == 1)
+                copy = nc.vector.tensor_copy if on_vector else nc.scalar.copy
+                copy(out=result[:], in_=part[:])
+                rows = out.rearrange("(a p) b -> p a b", p=P)[:, s * per : (s + 1) * per, :]
+                nc.sync.dma_start(out=rows[:, :, c * CHUNK : (c + 1) * CHUNK], in_=result[:])
 
         for i in range(LEAD):
             gather(i)
@@ -218,13 +244,15 @@ def tile_list_group_spread_kernel(tc, xt, fa, fb, wa_words, wa_scales, wb_words,
                 gather(i + LEAD)
             if i < n_items:
                 linear(i)
-            if i in closes:
-                round_mean(closes[i])
+            if i - LAG_M in closes:
+                round_mean(closes[i - LAG_M])
             if i - LAG_U in closes:
                 round_spread(closes[i - LAG_U])
             if i < n_items:
                 squares(i)
+            if i - LAG_U in closes:
+                product_mean(closes[i - LAG_U])
             if i - LAG_W in closes:
-                product(closes[i - LAG_W])
+                product_spread(closes[i - LAG_W])
             if i - LAG_S in closes:
                 store(closes[i - LAG_S])

@@ -21,52 +21,52 @@ ALU = mybir.AluOpType
 P = 128
 PACK = 4
 GROUP = J // B
+PER_COLUMN = 16
 CHUNK = 128
-HALF = 256
-
-
-G_BUFS = 3
-M_BUFS = 5
+N_CHUNKS = B // CHUNK
+LAST = N_CHUNKS - 1
+HALF = B // 2
+RUN = 4
 LEAD = 2
-ON_VECTOR = {1: 2, 4: 2}
-SPLIT_LAST = 1
-SPLIT_OUT = (3,)
-LAG_U = 1
-LAG_W = 2
-LAG_S = 3
-ORDER = 1
-WORDS_ON_VECTOR = ()
-OUT_ON_VECTOR = ()
-LAG_M = 1
-T_BUFS = 1
+
+ITEMS = (
+    [((t,), h * HALF, HALF) for t in (0, 1) for h in (0, 1)]
+    + [((2, 3), c * CHUNK, CHUNK) for c in range(LAST)]
+    + [((t,), LAST * CHUNK, CHUNK) for t in (2, 3)]
+)
+CLOSES = {i: item[1] // CHUNK for i, item in enumerate(ITEMS) if PACK - 1 in item[0]}
+ON_VECTOR = {1: HALF, 4: HALF, 6: HALF // 4}
 
 
 def tile_list_group_spread_kernel(tc, xt, fa, fb, wa_words, wa_scales, wb_words, wb_scales, offs, out):
     nc = tc.nc
     with ExitStack() as ctx:
         held = ctx.enter_context(tc.tile_pool(name="held", bufs=1))
-        gathered = ctx.enter_context(tc.tile_pool(name="gathered", bufs=G_BUFS))
-        ring = ctx.enter_context(tc.tile_pool(name="ring", bufs=M_BUFS))
-        late = ctx.enter_context(tc.tile_pool(name="late", bufs=4))
-        sums = ctx.enter_context(tc.psum_pool(name="sums", bufs=1))
-        turn = ctx.enter_context(tc.psum_pool(name="turn", bufs=T_BUFS))
-        psum = ctx.enter_context(tc.psum_pool(name="psum", bufs=4 - T_BUFS))
+        gathered = ctx.enter_context(tc.tile_pool(name="gathered", bufs=LEAD + 1))
+        per_item = ctx.enter_context(tc.tile_pool(name="per_item", bufs=len(ITEMS)))
+        per_chunk = ctx.enter_context(tc.tile_pool(name="per_chunk", bufs=N_CHUNKS))
+        chunk_bank = ctx.enter_context(tc.psum_pool(name="chunk_bank", bufs=1))
+        word_bank = ctx.enter_context(tc.psum_pool(name="word_bank", bufs=2))
+        spare_bank = ctx.enter_context(tc.psum_pool(name="spare_bank", bufs=1))
 
-        offsets = held.tile([P, J // 16], U16, name="offsets")
+        offsets = held.tile([P, J // PER_COLUMN], U16, name="offsets")
         planes = [held.tile([P, T], F32, name="plane%d" % t) for t in range(PACK)]
         ident = held.tile([P, P], F32, name="ident")
-        fb_t = held.tile([P, PACK], F32, name="fb_t")
+        fa_col = held.tile([P, PACK], F32, name="fa_col")
+        fb_col = held.tile([P, PACK], F32, name="fb_col")
+        fb_mean = held.tile([P, PACK], F32, name="fb_mean")
         fa_row = held.tile([P, K], F32, name="fa_row")
-        fb_quarter = held.tile([P, PACK], F32, name="fb_quarter")
         wa = held.tile([P, 2 * N], U8, name="wa", align_bytes=64)
         wb = held.tile([P, 4 * N], U8, name="wb", align_bytes=64)
-        wa_s = held.tile([P, N], U8, name="wa_s", align_bytes=64)
-        wb_s = held.tile([P, N], U8, name="wb_s", align_bytes=64)
+        wa_scale = held.tile([P, N], U8, name="wa_scale", align_bytes=64)
+        wb_scale = held.tile([P, N], U8, name="wb_scale", align_bytes=64)
         total = [held.tile([P, PACK, HALF], F32, name="total%d" % h) for h in range(2)]
-        spread = [sums.tile([P, PACK, P], F32, name="spread%d" % c) for c in range(B // CHUNK)]
+        last_spread = held.tile([P, PACK, CHUNK], F32, name="last_spread")
+        spread = [chunk_bank.tile([P, PACK, P], F32, name="spread%d" % c, tag="bank%d" % c) for c in range(LAST)]
 
         xt_planes = xt.rearrange("(p t) n -> t p n", t=PACK)
-        nc.scalar.dma_start(out=fb_t[:], in_=fb.rearrange("(p t) o -> p (t o)", t=PACK))
+        nc.scalar.dma_start(out=fb_col[:], in_=fb.rearrange("(p t) o -> p (t o)", t=PACK))
+        nc.scalar.dma_start(out=fa_col[:], in_=fa.rearrange("(p t) o -> p (t o)", t=PACK))
         nc.sync.dma_start(offsets[:], offs)
         for t in range(PACK):
             nc.sync.dma_start(out=planes[t][:], in_=xt_planes[t])
@@ -74,55 +74,40 @@ def tile_list_group_spread_kernel(tc, xt, fa, fb, wa_words, wa_scales, wb_words,
         nc.sync.dma_start(out=wb[:].bitcast(I32), in_=wb_words[0].rearrange("p n t -> p (n t)").bitcast(I32))
         nc.sync.dma_start(out=fa_row[:], in_=fa.rearrange("k o -> (k o)").partition_broadcast(P))
         make_identity(nc, ident[:])
-        for plane, scales in ((wa_s, wa_scales), (wb_s, wb_scales)):
-            nc.gpsimd.memset(plane[:].bitcast(I32), 0)
-            for q in range(4):
+        for scale_tile, scale_rows in ((wa_scale, wa_scales), (wb_scale, wb_scales)):
+            nc.gpsimd.memset(scale_tile[:].bitcast(I32), 0)
+            for s in range(4):
                 nc.sync.dma_start(
-                    out=plane[32 * q : 32 * q + 4, :].bitcast(I32),
-                    in_=scales[0, 4 * q : 4 * q + 4, :].bitcast(I32),
+                    out=scale_tile[32 * s : 32 * s + 4, :].bitcast(I32),
+                    in_=scale_rows[0, 4 * s : 4 * s + 4, :].bitcast(I32),
                 )
-        nc.scalar.activation(out=fb_quarter[:], in_=fb_t[:], func=ACT.Copy, scale=0.25)
+        nc.scalar.activation(out=fb_mean[:], in_=fb_col[:], func=ACT.Copy, scale=1.0 / GROUP)
 
-        halves = [((t,), h * HALF, HALF) for t in range(2) for h in range(2)]
-        quarters = [((2, 3), c * CHUNK, CHUNK) for c in range(4)]
-        if SPLIT_LAST:
-            quarters = quarters[:3] + [((2,), 3 * CHUNK, CHUNK), ((3,), 3 * CHUNK, CHUNK)]
-        items = [
-            halves[:3] + quarters[:2] + halves[3:] + quarters[2:],
-            halves + quarters,
-            halves[:3] + quarters[:1] + halves[3:] + quarters[1:],
-        ][ORDER]
-        n_items = len(items)
-        closes = {i: items[i][1] // CHUNK for i in range(n_items) if 3 in items[i][0]}
         made = {}
 
         def gather(i):
-            ts, b0, nb = items[i]
+            ts, b0, nb = ITEMS[i]
             g = gathered.tile([P, GROUP * nb * len(ts)], F32, name="g%d" % i, tag="g")
-            share = ON_VECTOR.get(i, 0)
-            if len(ts) == 1:
-                cut = nb - share * CHUNK
-                parts = [(ts[0], 0, cut, False), (ts[0], cut, nb, True)]
-            else:
-                parts = [(t, 0, nb, s >= len(ts) - share) for s, t in enumerate(ts)]
-            for t, lo, hi, on_vector in parts:
-                if lo == hi:
-                    continue
-                at = (t - ts[0]) * nb
-                dst = g[:, (at + lo) * GROUP : (at + hi) * GROUP]
-                window = planes[t][:].indirect(offsets[:, (b0 + lo) * GROUP // 16 : (b0 + hi) * GROUP // 16])
-                if on_vector:
-                    nc.vector.tensor_copy(out=dst, in_=window)
-                else:
-                    nc.scalar.activation(out=dst, in_=window, func=ACT.Copy)
+            on_scalar = nb * len(ts) - ON_VECTOR.get(i, 0)
+            for s, t in enumerate(ts):
+                cut = min(max(on_scalar - s * nb, 0), nb)
+                for lo, hi in ((0, cut), (cut, nb)):
+                    if lo == hi:
+                        continue
+                    dst = g[:, (s * nb + lo) * GROUP : (s * nb + hi) * GROUP]
+                    entries = offsets[:, (b0 + lo) * GROUP // PER_COLUMN : (b0 + hi) * GROUP // PER_COLUMN]
+                    if hi <= cut:
+                        nc.scalar.activation(out=dst, in_=planes[t][:].indirect(entries), func=ACT.Copy)
+                    else:
+                        nc.vector.tensor_copy(out=dst, in_=planes[t][:].indirect(entries))
             made["g", i] = g
 
-        def linear(i):
-            ts, b0, nb = items[i]
+        def sums_and_differences(i):
+            ts, b0, nb = ITEMS[i]
             g = made["g", i][:].rearrange("p (b j) -> p b j", j=GROUP)
-            both = ring.tile([P, nb * len(ts), 2], F32, name="both%d" % i, tag="both")
-            diff = ring.tile([P, nb * len(ts), 2], F32, name="diff%d" % i, tag="diff")
-            odd = ring.tile([P, nb * len(ts)], F32, name="odd%d" % i, tag="odd")
+            both = per_item.tile([P, nb * len(ts), 2], F32, name="both%d" % i, tag="both")
+            diff = per_item.tile([P, nb * len(ts), 2], F32, name="diff%d" % i, tag="diff")
+            odd = per_item.tile([P, nb * len(ts)], F32, name="odd%d" % i, tag="odd")
             nc.vector.tensor_tensor(out=both[:], in0=g[:, :, 0:2], in1=g[:, :, 2:4], op=ALU.add)
             nc.vector.tensor_tensor(out=diff[:], in0=g[:, :, 0:2], in1=g[:, :, 2:4], op=ALU.subtract)
             nc.vector.tensor_tensor(out=odd[:], in0=both[:, :, 0], in1=both[:, :, 1], op=ALU.subtract)
@@ -136,16 +121,19 @@ def tile_list_group_spread_kernel(tc, xt, fa, fb, wa_words, wa_scales, wb_words,
             made["odd", i] = odd
 
         def squares(i):
-            ts, b0, nb = items[i]
-            diff_sq = ring.tile([P, nb * len(ts), 2], F32, name="diff_sq%d" % i, tag="diff_sq")
-            odd_sq = ring.tile([P, nb * len(ts)], F32, name="odd_sq%d" % i, tag="odd_sq")
-            nc.scalar.activation(out=diff_sq[:], in_=made["diff", i][:], func=ACT.Square, scale=math.sqrt(0.125))
-            nc.scalar.activation(out=odd_sq[:], in_=made["odd", i][:], func=ACT.Square, scale=0.25)
+            ts, b0, nb = ITEMS[i]
+            diff_sq = per_item.tile([P, nb * len(ts), 2], F32, name="diff_sq%d" % i, tag="diff_sq")
+            odd_sq = per_item.tile([P, nb * len(ts)], F32, name="odd_sq%d" % i, tag="odd_sq")
+            nc.scalar.activation(out=diff_sq[:], in_=made["diff", i][:], func=ACT.Square, scale=math.sqrt(1.0 / 8))
+            nc.scalar.activation(out=odd_sq[:], in_=made["odd", i][:], func=ACT.Square, scale=math.sqrt(1.0 / 16))
             for s in range(nb * len(ts) // CHUNK):
                 t = ts[s * CHUNK // nb]
                 c = (b0 + s * CHUNK % nb) // CHUNK
                 cols = slice(s * CHUNK, (s + 1) * CHUNK)
                 terms = (diff_sq[:, cols, 0], diff_sq[:, cols, 1], odd_sq[:, cols])
+                if c == LAST:
+                    made["last_terms", i] = (t, terms)
+                    continue
                 for n, term in enumerate(terms):
                     nc.tensor.matmul(
                         out=spread[c][:, t, :],
@@ -156,103 +144,107 @@ def tile_list_group_spread_kernel(tc, xt, fa, fb, wa_words, wa_scales, wb_words,
                         is_transpose=True,
                     )
 
-        def quantize(rounded, key, c):
-            codes = late.tile([P, CHUNK], U32, name="codes_%s%d" % (key, c), tag="codes_" + key, align_bytes=64)
-            scales = late.tile([P, CHUNK], U8, name="scales_%s%d" % (key, c), tag="scales_" + key, align_bytes=64)
-            nc.vector.quantize_mx(out=codes[:].bitcast(FP8X4), scales=scales[:], in_=rounded[:])
-            return codes, scales
+        def add_last_terms(i):
+            t, terms = made["last_terms", i]
+            part = per_chunk.tile([P, CHUNK], F32, name="part%d" % t, tag="part")
+            nc.vector.tensor_tensor(out=part[:], in0=terms[0], in1=terms[1], op=ALU.add)
+            nc.vector.tensor_tensor(out=last_spread[:, t, :], in0=part[:], in1=terms[2], op=ALU.add)
+
+        def scale_and_interleave(key, c, values, factor):
+            rounded = per_chunk.tile([P, CHUNK * PACK], BF16, name="%s%d" % (key, c), tag=key, align_bytes=64)
+            nc.vector.tensor_tensor(
+                out=rounded[:].rearrange("p (r i t) -> p r t i", i=RUN, t=PACK),
+                in0=values.rearrange("p t (r i) -> p r t i", i=RUN),
+                in1=factor[:].unsqueeze(1).unsqueeze(3).to_broadcast([P, CHUNK // RUN, PACK, RUN]),
+                op=ALU.mult,
+            )
+            made[key, c] = rounded
 
         def round_mean(c):
             b0 = c * CHUNK
-            rounded = late.tile([P, CHUNK * PACK], BF16, name="v%d" % c, tag="v", align_bytes=64)
-            src = total[b0 // HALF][:, :, b0 % HALF : b0 % HALF + CHUNK]
-            nc.vector.tensor_tensor(
-                out=rounded[:].rearrange("p (c i t) -> p c t i", i=2, t=PACK),
-                in0=src.rearrange("p t (c i) -> p c t i", i=2),
-                in1=fb_quarter[:].unsqueeze(1).unsqueeze(3).to_broadcast([P, CHUNK // 2, PACK, 2]),
-                op=ALU.mult,
-            )
-            made["v", c] = rounded
+            scale_and_interleave("v", c, total[b0 // HALF][:, :, b0 % HALF : b0 % HALF + CHUNK], fb_mean)
 
         def round_spread(c):
-            pairs = late.tile([P, 2, P, 2], BF16, name="pairs%d" % c, tag="pairs")
+            if c == LAST:
+                scale_and_interleave("u", c, last_spread[:], fa_col)
+                return
+            pairs = per_chunk.tile([P, 2, P, 2], BF16, name="pairs%d" % c, tag="pairs")
             nc.vector.tensor_tensor(
                 out=pairs[:],
-                in0=spread[c][:].rearrange("b (u e) p -> b u p e", e=2),
-                in1=fa_row[:].rearrange("b (p u e) -> b u p e", u=2, e=2),
+                in0=spread[c][:].rearrange("b (w e) p -> b w p e", e=2),
+                in1=fa_row[:].rearrange("b (p w e) -> b w p e", w=2, e=2),
                 op=ALU.mult,
             )
-            words = pairs[:].rearrange("b u p e -> b u (p e)").bitcast(F32)
-            turned = turn.tile([P, PACK, P], F32, name="turned%d" % c, tag="turned")
-            for u in range(2):
-                nc.tensor.transpose(turned[:, u, :], words[:, u, :], ident[:])
+            words = pairs[:].rearrange("b w p e -> b w (p e)").bitcast(F32)
+            turned = word_bank.tile([P, 2, P], F32, name="turned%d" % c, tag="turned")
+            for w in range(2):
+                nc.tensor.transpose(turned[:, w, :], words[:, w, :], ident[:])
             made["turned", c] = turned
 
-        def product_mean(c):
-            codes, scales = quantize(made["v", c], "v", c)
-            n_parts = 2 if c in SPLIT_OUT else 1
-            per = N // P // n_parts
-            acc = [psum.tile([P, per, CHUNK], F32, name="acc%d_%d" % (c, s), tag="acc") for s in range(n_parts)]
+        def quantize_and_multiply(key, c, weight, word_bytes, word_dtype, weight_scale, first):
+            codes = per_chunk.tile([P, CHUNK], U32, name="codes_%s%d" % (key, c), tag="codes_" + key, align_bytes=64)
+            scales = per_chunk.tile([P, CHUNK], U8, name="scales_%s%d" % (key, c), tag="scales_" + key, align_bytes=64)
+            nc.vector.quantize_mx(out=codes[:].bitcast(FP8X4), scales=scales[:], in_=made[key, c][:])
+            banks = made["banks", c]
+            per_bank = N // P // len(banks)
             for a in range(N // P):
                 nc.tensor.matmul_mx(
-                    out=acc[a // per][:, a % per, :],
-                    lhsT=wb[:, 4 * P * a : 4 * P * (a + 1)].bitcast(FP8X4),
-                    lhsT_scale=wb_s[:, P * a : P * (a + 1)],
+                    out=banks[a // per_bank][:, a % per_bank, :],
+                    lhsT=weight[:, word_bytes * P * a : word_bytes * P * (a + 1)].bitcast(word_dtype),
+                    lhsT_scale=weight_scale[:, P * a : P * (a + 1)],
                     rhs=codes[:].bitcast(FP8X4),
                     rhs_scale=scales[:],
-                    start=(a % per == 0),
-                    stop=False,
+                    start=(first and a % per_bank == 0),
+                    stop=(not first and a % per_bank == per_bank - 1),
                 )
-            made["acc", c] = acc
+
+        def product_mean(c):
+            per_bank = N // P // (2 if c == LAST else 1)
+            banks = [chunk_bank.tile([P, per_bank, CHUNK], F32, name="product%d" % c, tag="bank%d" % c)]
+            if c == LAST:
+                banks.append(spare_bank.tile([P, per_bank, CHUNK], F32, name="product_spare"))
+            made["banks", c] = banks
+            quantize_and_multiply("v", c, wb, 4, FP8X4, wb_scale, True)
 
         def product_spread(c):
-            rounded = late.tile([P, CHUNK * PACK], BF16, name="u%d" % c, tag="u", align_bytes=64)
-            copy = nc.vector.tensor_copy if c in WORDS_ON_VECTOR else nc.scalar.copy
-            copy(
-                out=rounded[:].bitcast(F32).rearrange("p (b u) -> p b u", u=2),
-                in_=made["turned", c][:, 0:2, :].rearrange("p u b -> p b u"),
-            )
-            codes, scales = quantize(rounded, "u", c)
-            acc = made["acc", c]
-            per = N // P // len(acc)
-            for a in range(N // P):
-                nc.tensor.matmul_mx(
-                    out=acc[a // per][:, a % per, :],
-                    lhsT=wa[:, 2 * P * a : 2 * P * (a + 1)].bitcast(FP4X4),
-                    lhsT_scale=wa_s[:, P * a : P * (a + 1)],
-                    rhs=codes[:].bitcast(FP8X4),
-                    rhs_scale=scales[:],
-                    start=False,
-                    stop=(a % per == per - 1),
+            if c != LAST:
+                rounded = per_chunk.tile([P, CHUNK * PACK], BF16, name="u%d" % c, tag="u", align_bytes=64)
+                nc.scalar.copy(
+                    out=rounded[:].bitcast(F32).rearrange("p (b w) -> p b w", w=2),
+                    in_=made["turned", c][:].rearrange("p w b -> p b w"),
                 )
+                made["u", c] = rounded
+            quantize_and_multiply("u", c, wa, 2, FP4X4, wa_scale, False)
 
         def store(c):
-            acc = made["acc", c]
-            per = N // P // len(acc)
-            for s, part in enumerate(acc):
-                result = late.tile([P, per, CHUNK], F32, name="result%d_%d" % (c, s), tag="result")
-                on_vector = (c in OUT_ON_VECTOR) != (s == 1)
-                copy = nc.vector.tensor_copy if on_vector else nc.scalar.copy
-                copy(out=result[:], in_=part[:])
-                rows = out.rearrange("(a p) b -> p a b", p=P)[:, s * per : (s + 1) * per, :]
-                nc.sync.dma_start(out=rows[:, :, c * CHUNK : (c + 1) * CHUNK], in_=result[:])
+            banks = made["banks", c]
+            per_bank = N // P // len(banks)
+            for s, bank in enumerate(banks):
+                result = per_chunk.tile([P, per_bank, CHUNK], F32, name="result%d_%d" % (c, s), tag="result")
+                copy = nc.scalar.copy if s == 0 else nc.vector.tensor_copy
+                copy(out=result[:], in_=bank[:])
+                queue = nc.scalar if (c == LAST and s == 0) else nc.sync
+                rows = out.rearrange("(a p) b -> p a b", p=P)[:, s * per_bank : (s + 1) * per_bank, :]
+                queue.dma_start(out=rows[:, :, c * CHUNK : (c + 1) * CHUNK], in_=result[:])
 
         for i in range(LEAD):
             gather(i)
-        for i in range(n_items + LAG_S):
-            if i + LEAD < n_items:
+        for i in range(len(ITEMS) + 4):
+            if i + LEAD < len(ITEMS):
                 gather(i + LEAD)
-            if i < n_items:
-                linear(i)
-            if i - LAG_M in closes:
-                round_mean(closes[i - LAG_M])
-            if i - LAG_U in closes:
-                round_spread(closes[i - LAG_U])
-            if i < n_items:
+            if i < len(ITEMS):
+                sums_and_differences(i)
+            if ("last_terms", i - 1) in made:
+                add_last_terms(i - 1)
+            if i - 1 in CLOSES:
+                round_mean(CLOSES[i - 1])
+            if i - 2 in CLOSES:
+                round_spread(CLOSES[i - 2])
+            if i < len(ITEMS):
                 squares(i)
-            if i - LAG_U in closes:
-                product_mean(closes[i - LAG_U])
-            if i - LAG_W in closes:
-                product_spread(closes[i - LAG_W])
-            if i - LAG_S in closes:
-                store(closes[i - LAG_S])
+            if i - 2 in CLOSES:
+                product_mean(CLOSES[i - 2])
+            if i - 3 in CLOSES:
+                product_spread(CLOSES[i - 3])
+            if i - 4 in CLOSES:
+                store(CLOSES[i - 4])

@@ -66,10 +66,11 @@ def tile_list_group_spread_kernel(tc, xt, fa, fb, wa_words, wa_scales, wb_words,
 
         xt_planes = xt.rearrange("(p t) n -> t p n", t=PACK)
         nc.scalar.dma_start(out=fb_col[:], in_=fb.rearrange("(p t) o -> p (t o)", t=PACK))
-        nc.scalar.dma_start(out=fa_col[:], in_=fa.rearrange("(p t) o -> p (t o)", t=PACK))
+        nc.sync.dma_start(out=planes[0][:], in_=xt_planes[0])
         nc.sync.dma_start(offsets[:], offs)
-        for t in range(PACK):
+        for t in range(1, PACK):
             nc.sync.dma_start(out=planes[t][:], in_=xt_planes[t])
+        nc.sync.dma_start(out=fa_col[:], in_=fa.rearrange("(p t) o -> p (t o)", t=PACK))
         nc.sync.dma_start(out=wa[:].bitcast(I32), in_=wa_words[0].bitcast(I32))
         nc.sync.dma_start(out=wb[:].bitcast(I32), in_=wb_words[0].rearrange("p n t -> p (n t)").bitcast(I32))
         nc.sync.dma_start(out=fa_row[:], in_=fa.rearrange("k o -> (k o)").partition_broadcast(P))

import math
from contextlib import ExitStack

import concourse.mybir as mybir
from concourse.masks import make_identity

K, T, J, B, N = 512, 2048, 2048, 512, 512
FLOPS = 2 * 2 * K * N * B

F32 = mybir.dt.float32
BF16 = mybir.dt.bfloat16
I32 = mybir.dt.int32
U32 = mybir.dt.uint32
U16 = mybir.dt.uint16
U8 = mybir.dt.uint8
FP8X4 = mybir.dt.float8_e4m3fn_x4
FP4X4 = mybir.dt.float4_e2m1fn_x4
ACT = mybir.ActivationFunctionType
ALU = mybir.AluOpType

P = 128
PACK = 4
GROUP = J // B
PER_COLUMN = 16
CHUNK = 128
N_CHUNKS = B // CHUNK
LAST = N_CHUNKS - 1
HALF = B // 2
RUN = 4
LEAD = 2

ITEMS = (
    [((t,), h * HALF, HALF) for t in (0, 1) for h in (0, 1)]
    + [((2, 3), c * CHUNK, CHUNK) for c in range(LAST)]
    + [((t,), LAST * CHUNK, CHUNK) for t in (2, 3)]
)
CLOSES = {i: item[1] // CHUNK for i, item in enumerate(ITEMS) if PACK - 1 in item[0]}
ON_VECTOR = {1: HALF, 4: HALF, 6: HALF // 4}


def tile_list_group_spread_kernel(tc, xt, fa, fb, wa_words, wa_scales, wb_words, wb_scales, offs, out):
    nc = tc.nc
    with ExitStack() as ctx:
        held = ctx.enter_context(tc.tile_pool(name="held", bufs=1))
        gathered = ctx.enter_context(tc.tile_pool(name="gathered", bufs=LEAD + 1))
        per_item = ctx.enter_context(tc.tile_pool(name="per_item", bufs=len(ITEMS)))
        per_chunk = ctx.enter_context(tc.tile_pool(name="per_chunk", bufs=N_CHUNKS))
        chunk_bank = ctx.enter_context(tc.psum_pool(name="chunk_bank", bufs=1))
        word_bank = ctx.enter_context(tc.psum_pool(name="word_bank", bufs=2))
        spare_bank = ctx.enter_context(tc.psum_pool(name="spare_bank", bufs=1))

        offsets = held.tile([P, J // PER_COLUMN], U16, name="offsets")
        planes = [held.tile([P, T], F32, name="plane%d" % t) for t in range(PACK)]
        ident = held.tile([P, P], F32, name="ident")
        fa_col = held.tile([P, PACK], F32, name="fa_col")
        fb_col = held.tile([P, PACK], F32, name="fb_col")
        fb_mean = held.tile([P, PACK], F32, name="fb_mean")
        fa_row = held.tile([P, K], F32, name="fa_row")
        wa = held.tile([P, 2 * N], U8, name="wa", align_bytes=64)
        wb = held.tile([P, 4 * N], U8, name="wb", align_bytes=64)
        wa_scale = held.tile([P, N], U8, name="wa_scale", align_bytes=64)
        wb_scale = held.tile([P, N], U8, name="wb_scale", align_bytes=64)
        total = [held.tile([P, PACK, HALF], F32, name="total%d" % h) for h in range(2)]
        last_spread = held.tile([P, PACK, CHUNK], F32, name="last_spread")
        spread = [chunk_bank.tile([P, PACK, P], F32, name="spread%d" % c, tag="bank%d" % c) for c in range(LAST)]

        xt_planes = xt.rearrange("(p t) n -> t p n", t=PACK)
        nc.scalar.dma_start(out=fb_col[:], in_=fb.rearrange("(p t) o -> p (t o)", t=PACK))
        nc.sync.dma_start(out=planes[0][:], in_=xt_planes[0])
        nc.sync.dma_start(offsets[:], offs)
        for t in range(1, PACK):
            nc.sync.dma_start(out=planes[t][:], in_=xt_planes[t])
        nc.sync.dma_start(out=fa_col[:], in_=fa.rearrange("(p t) o -> p (t o)", t=PACK))
        nc.sync.dma_start(out=wa[:].bitcast(I32), in_=wa_words[0].bitcast(I32))
        nc.sync.dma_start(out=wb[:].bitcast(I32), in_=wb_words[0].rearrange("p n t -> p (n t)").bitcast(I32))
        nc.sync.dma_start(out=fa_row[:], in_=fa.rearrange("k o -> (k o)").partition_broadcast(P))
        make_identity(nc, ident[:])
        for scale_tile, scale_rows in ((wa_scale, wa_scales), (wb_scale, wb_scales)):
            nc.gpsimd.memset(scale_tile[:].bitcast(I32), 0)
            for s in range(4):
                nc.sync.dma_start(
                    out=scale_tile[32 * s : 32 * s + 4, :].bitcast(I32),
                    in_=scale_rows[0, 4 * s : 4 * s + 4, :].bitcast(I32),
                )
        nc.scalar.activation(out=fb_mean[:], in_=fb_col[:], func=ACT.Copy, scale=1.0 / GROUP)

        made = {}

        def gather(i):
            ts, b0, nb = ITEMS[i]
            g = gathered.tile([P, GROUP * nb * len(ts)], F32, name="g%d" % i, tag="g")
            on_scalar = nb * len(ts) - ON_VECTOR.get(i, 0)
            for s, t in enumerate(ts):
                cut = min(max(on_scalar - s * nb, 0), nb)
                for lo, hi in ((0, cut), (cut, nb)):
                    if lo == hi:
                        continue
                    dst = g[:, (s * nb + lo) * GROUP : (s * nb + hi) * GROUP]
                    entries = offsets[:, (b0 + lo) * GROUP // PER_COLUMN : (b0 + hi) * GROUP // PER_COLUMN]
                    if hi <= cut:
                        nc.scalar.activation(out=dst, in_=planes[t][:].indirect(entries), func=ACT.Copy)
                    else:
                        nc.vector.tensor_copy(out=dst, in_=planes[t][:].indirect(entries))
            made["g", i] = g

        def sums_and_differences(i):
            ts, b0, nb = ITEMS[i]
            g = made["g", i][:].rearrange("p (b j) -> p b j", j=GROUP)
            both = per_item.tile([P, nb * len(ts), 2], F32, name="both%d" % i, tag="both")
            diff = per_item.tile([P, nb * len(ts), 2], F32, name="diff%d" % i, tag="diff")
            odd = per_item.tile([P, nb * len(ts)], F32, name="odd%d" % i, tag="odd")
            nc.vector.tensor_tensor(out=both[:], in0=g[:, :, 0:2], in1=g[:, :, 2:4], op=ALU.add)
            nc.vector.tensor_tensor(out=diff[:], in0=g[:, :, 0:2], in1=g[:, :, 2:4], op=ALU.subtract)
            nc.vector.tensor_tensor(out=odd[:], in0=both[:, :, 0], in1=both[:, :, 1], op=ALU.subtract)
            nc.vector.tensor_tensor(
                out=total[b0 // HALF][:, ts[0] : ts[-1] + 1, b0 % HALF : b0 % HALF + nb],
                in0=both[:, :, 0].rearrange("p (t b) -> p t b", t=len(ts)),
                in1=both[:, :, 1].rearrange("p (t b) -> p t b", t=len(ts)),
                op=ALU.add,
            )
            made["diff", i] = diff
            made["odd", i] = odd

        def squares(i):
            ts, b0, nb = ITEMS[i]
            diff_sq = per_item.tile([P, nb * len(ts), 2], F32, name="diff_sq%d" % i, tag="diff_sq")
            odd_sq = per_item.tile([P, nb * len(ts)], F32, name="odd_sq%d" % i, tag="odd_sq")
            nc.scalar.activation(out=diff_sq[:], in_=made["diff", i][:], func=ACT.Square, scale=math.sqrt(1.0 / 8))
            nc.scalar.activation(out=odd_sq[:], in_=made["odd", i][:], func=ACT.Square, scale=math.sqrt(1.0 / 16))
            for s in range(nb * len(ts) // CHUNK):
                t = ts[s * CHUNK // nb]
                c = (b0 + s * CHUNK % nb) // CHUNK
                cols = slice(s * CHUNK, (s + 1) * CHUNK)
                terms = (diff_sq[:, cols, 0], diff_sq[:, cols, 1], odd_sq[:, cols])
                if c == LAST:
                    made["last_terms", i] = (t, terms)
                    continue
                for n, term in enumerate(terms):
                    nc.tensor.matmul(
                        out=spread[c][:, t, :],
                        lhsT=term,
                        rhs=ident[:],
                        start=(n == 0),
                        stop=(n == len(terms) - 1),
                        is_transpose=True,
                    )

        def add_last_terms(i):
            t, terms = made["last_terms", i]
            part = per_chunk.tile([P, CHUNK], F32, name="part%d" % t, tag="part")
            nc.vector.tensor_tensor(out=part[:], in0=terms[0], in1=terms[1], op=ALU.add)
            nc.vector.tensor_tensor(out=last_spread[:, t, :], in0=part[:], in1=terms[2], op=ALU.add)

        def scale_and_interleave(key, c, values, factor):
            rounded = per_chunk.tile([P, CHUNK * PACK], BF16, name="%s%d" % (key, c), tag=key, align_bytes=64)
            nc.vector.tensor_tensor(
                out=rounded[:].rearrange("p (r i t) -> p r t i", i=RUN, t=PACK),
                in0=values.rearrange("p t (r i) -> p r t i", i=RUN),
                in1=factor[:].unsqueeze(1).unsqueeze(3).to_broadcast([P, CHUNK // RUN, PACK, RUN]),
                op=ALU.mult,
            )
            made[key, c] = rounded

        def round_mean(c):
            b0 = c * CHUNK
            scale_and_interleave("v", c, total[b0 // HALF][:, :, b0 % HALF : b0 % HALF + CHUNK], fb_mean)

        def round_spread(c):
            if c == LAST:
                scale_and_interleave("u", c, last_spread[:], fa_col)
                return
            pairs = per_chunk.tile([P, 2, P, 2], BF16, name="pairs%d" % c, tag="pairs")
            nc.vector.tensor_tensor(
                out=pairs[:],
                in0=spread[c][:].rearrange("b (w e) p -> b w p e", e=2),
                in1=fa_row[:].rearrange("b (p w e) -> b w p e", w=2, e=2),
                op=ALU.mult,
            )
            words = pairs[:].rearrange("b w p e -> b w (p e)").bitcast(F32)
            turned = word_bank.tile([P, 2, P], F32, name="turned%d" % c, tag="turned")
            for w in range(2):
                nc.tensor.transpose(turned[:, w, :], words[:, w, :], ident[:])
            made["turned", c] = turned

        def quantize_and_multiply(key, c, weight, word_bytes, word_dtype, weight_scale, first):
            codes = per_chunk.tile([P, CHUNK], U32, name="codes_%s%d" % (key, c), tag="codes_" + key, align_bytes=64)
            scales = per_chunk.tile([P, CHUNK], U8, name="scales_%s%d" % (key, c), tag="scales_" + key, align_bytes=64)
            nc.vector.quantize_mx(out=codes[:].bitcast(FP8X4), scales=scales[:], in_=made[key, c][:])
            banks = made["banks", c]
            per_bank = N // P // len(banks)
            for a in range(N // P):
                nc.tensor.matmul_mx(
                    out=banks[a // per_bank][:, a % per_bank, :],
                    lhsT=weight[:, word_bytes * P * a : word_bytes * P * (a + 1)].bitcast(word_dtype),
                    lhsT_scale=weight_scale[:, P * a : P * (a + 1)],
                    rhs=codes[:].bitcast(FP8X4),
                    rhs_scale=scales[:],
                    start=(first and a % per_bank == 0),
                    stop=(not first and a % per_bank == per_bank - 1),
                )

        def product_mean(c):
            per_bank = N // P // (2 if c == LAST else 1)
            banks = [chunk_bank.tile([P, per_bank, CHUNK], F32, name="product%d" % c, tag="bank%d" % c)]
            if c == LAST:
                banks.append(spare_bank.tile([P, per_bank, CHUNK], F32, name="product_spare"))
            made["banks", c] = banks
            quantize_and_multiply("v", c, wb, 4, FP8X4, wb_scale, True)

        def product_spread(c):
            if c != LAST:
                rounded = per_chunk.tile([P, CHUNK * PACK], BF16, name="u%d" % c, tag="u", align_bytes=64)
                nc.scalar.copy(
                    out=rounded[:].bitcast(F32).rearrange("p (b w) -> p b w", w=2),
                    in_=made["turned", c][:].rearrange("p w b -> p b w"),
                )
                made["u", c] = rounded
            quantize_and_multiply("u", c, wa, 2, FP4X4, wa_scale, False)

        def store(c):
            banks = made["banks", c]
            per_bank = N // P // len(banks)
            for s, bank in enumerate(banks):
                result = per_chunk.tile([P, per_bank, CHUNK], F32, name="result%d_%d" % (c, s), tag="result")
                copy = nc.scalar.copy if s == 0 else nc.vector.tensor_copy
                copy(out=result[:], in_=bank[:])
                queue = nc.scalar if (c == LAST and s == 0) else nc.sync
                rows = out.rearrange("(a p) b -> p a b", p=P)[:, s * per_bank : (s + 1) * per_bank, :]
                queue.dma_start(out=rows[:, :, c * CHUNK : (c + 1) * CHUNK], in_=result[:])

        for i in range(LEAD):
            gather(i)
        for i in range(len(ITEMS) + 4):
            if i + LEAD < len(ITEMS):
                gather(i + LEAD)
            if i < len(ITEMS):
                sums_and_differences(i)
            if ("last_terms", i - 1) in made:
                add_last_terms(i - 1)
            if i - 1 in CLOSES:
                round_mean(CLOSES[i - 1])
            if i - 2 in CLOSES:
                round_spread(CLOSES[i - 2])
            if i < len(ITEMS):
                squares(i)
            if i - 2 in CLOSES:
                product_mean(CLOSES[i - 2])
            if i - 3 in CLOSES:
                product_spread(CLOSES[i - 3])
            if i - 4 in CLOSES:
                store(CLOSES[i - 4])
